import numpy as np
import ml_dtypes


def mxq(x, axis, fmt="e4m3"):
    dtype, down = {"e4m3": (ml_dtypes.float8_e4m3fn, 7), "e5m2": (ml_dtypes.float8_e5m2, 14)}[fmt]
    v = np.moveaxis(np.asarray(x, np.float32).astype(ml_dtypes.bfloat16).astype(np.float64), axis, -1)
    blocks = v.reshape(v.shape[:-1] + (-1, 32))
    amax = np.abs(blocks).max(-1, keepdims=True)
    byte = np.maximum(np.where(amax > 0, np.frexp(amax)[1] - 1 + 127, 0) - down, 1)
    scale = np.exp2(byte - 127.0)
    codes = (blocks / scale).astype(np.float32).astype(dtype).astype(np.float64)
    return np.moveaxis((codes * scale).reshape(v.shape), -1, axis)


WIDE = False


def mx_kscale(k):
    if not WIDE:
        return np.ones(k)
    levels = np.array([10, -10, 5, -5, 0])
    if k % 512:
        return np.exp2(np.random.permutation(np.resize(levels, k // 32))).repeat(32)
    a = np.empty((k // 512, 16))
    for p in range(k // 512):
        a[p, :8] = np.random.permutation(np.resize(levels, 8))
        for g in range(8):
            far = levels[np.abs(levels - a[p, g]) >= 10]
            a[p, g + 8] = far[np.random.randint(len(far))]
    return np.exp2(a.ravel()).repeat(32)


def f64(x):
    return np.asarray(x).astype(np.float64)


def striped(idx):
    return np.tile(idx.reshape(-1, 16).T, (8, 1)).astype(np.uint16)


def unstriped(offs):
    return offs[:16].T.reshape(-1).astype(np.int64)


E2M1 = np.array([0.0, 0.5, 1.0, 1.5, 2.0, 3.0, 4.0, 6.0, -0.0, -0.5, -1.0, -1.5, -2.0, -3.0, -4.0, -6.0])


def pack_weight(w, fmt):
    k, n = w.shape
    w = f64(np.asarray(w, np.float32).astype(ml_dtypes.bfloat16)).reshape(k // 32, 32, n)
    amax = np.abs(w).max(1)
    if fmt == "e4m3":
        byte = np.frexp(amax)[1] - 1 + 127 - 7
    else:
        mant, ex = np.frexp(amax / 6.0)
        byte = np.where(mant > 0.5, ex, ex - 1) + 127
    byte = np.clip(np.where(amax > 0, byte, 1), 1, 254)
    scaled = (w * np.exp2(127.0 - byte)[:, None, :]).reshape(k, n).astype(np.float32)
    by_word = np.ascontiguousarray(scaled.reshape(k // 512, 128, 4, n).transpose(0, 1, 3, 2))
    if fmt == "e4m3":
        words = by_word.astype(ml_dtypes.float8_e4m3fn).view(np.uint8)
    else:
        c = by_word.astype(ml_dtypes.float4_e2m1fn).view(np.uint8) & 0xF
        words = (c[..., 0::2] | (c[..., 1::2] << 4)).reshape(k // 512, 128, 2 * n)
    return np.ascontiguousarray(words), np.ascontiguousarray(byte.astype(np.uint8).reshape(k // 512, 16, n))


def unpack_weight(words, scales, fmt):
    g, _, n = scales.shape
    words = np.ascontiguousarray(words).reshape(g, 128, n, -1)
    if fmt == "e4m3":
        vals = words.view(ml_dtypes.float8_e4m3fn).astype(np.float64)
    else:
        nib = np.empty((g, 128, n, 4), np.uint8)
        nib[..., 0::2] = words & 0xF
        nib[..., 1::2] = words >> 4
        vals = E2M1[nib]
    vals = vals * np.repeat(np.exp2(scales.astype(np.float64) - 127.0), 8, axis=1)[..., None]
    return vals.transpose(0, 1, 3, 2).reshape(g * 512, n)


def gelu(v):
    return 0.5 * v * (1.0 + np.tanh(np.sqrt(2.0 / np.pi) * (v + 0.044715 * v**3)))


K, T, E, C, H, N = 2048, 640, 10, 128, 512, 256


def by_expert(wq, xq):
    return np.concatenate([wq[e].T @ xq[:, e * C:(e + 1) * C] for e in range(E)], axis=1)


def setup_inputs():
    n = np.random.standard_normal
    s = mx_kscale(K)
    u = mx_kscale(H)
    first = np.random.permutation(np.repeat(np.arange(E), T // E))
    second = (first + 1 + np.random.permutation(np.repeat(np.arange(E - 1), -(-T // (E - 1)))[:T])) % E
    while np.bincount(second, minlength=E).max() != T // E:
        load = np.bincount(second, minlength=E); hi, lo = int(load.argmax()), int(load.argmin())
        t = np.flatnonzero((second == hi) & (first != lo))[0]; second[t] = lo
    slot_token = np.empty(E * C, np.int64); pos = np.empty((2, T), np.int64); fill = np.zeros(E, np.int64)
    place = np.stack([np.random.permutation(C) for _ in range(E)])
    for r, deal in enumerate((first, second)):
        for t in np.random.permutation(T):
            e = deal[t]; j = e * C + place[e, fill[e]]; fill[e] += 1; slot_token[j] = t; pos[r, t] = j
    g = np.random.uniform(0.2, 0.8, T)
    x = pack_weight(n((K, T)) * s[:, None], "e4m3")
    w1 = pack_weight(n((K, H)) / np.sqrt(K) / s[:, None] * u, "e2m1")
    w2 = [pack_weight(m, "e4m3") for m in n((E, H, N)) / np.sqrt(H) / u[None, :, None]]
    return {
        "x_words": x[0],
        "x_scales": x[1],
        "w1_words": w1[0],
        "w1_scales": w1[1],
        "w2_words": np.stack([m[0] for m in w2]),
        "w2_scales": np.stack([m[1] for m in w2]),
        "gate": np.stack([np.tile(g, (128, 1)), np.tile(1.0 - g, (128, 1))]).astype(np.float32),
        "offs": striped(slot_token),
        "pos1": striped(pos[0]),
        "pos2": striped(pos[1]),
    }


def reference(x_words, x_scales, w1_words, w1_scales, w2_words, w2_scales, gate, offs, pos1, pos2):
    w1 = unpack_weight(w1_words, w1_scales, "e2m1")
    w2 = np.stack([unpack_weight(w2_words[e], w2_scales[e], "e4m3") for e in range(E)])
    idx = unstriped(offs)
    x = unpack_weight(x_words, x_scales, "e4m3")
    h = gelu(w1.T @ x)
    y = by_expert(w2, mxq(h[:, idx], 0, "e4m3"))
    out = sum(f64(gate[r, :1]) * y[:, unstriped(p)] for r, p in enumerate((pos1, pos2)))
    return out

@@ -1,0 +1,179 @@
+from contextlib import ExitStack
+
+import concourse.mybir as mybir
+
+K, T, E, C, H, N = 2048, 640, 10, 128, 512, 256
+S = E * C
+FLOPS = 2 * K * H * T + 2 * H * N * S
+
+F32 = mybir.dt.float32
+BF16 = mybir.dt.bfloat16
+I32 = mybir.dt.int32
+U32 = mybir.dt.uint32
+U16 = mybir.dt.uint16
+U8 = mybir.dt.uint8
+FP8X4 = mybir.dt.float8_e4m3fn_x4
+FP4X4 = mybir.dt.float4_e2m1fn_x4
+GELU = mybir.ActivationFunctionType.Gelu_apprx_tanh
+MULT = mybir.AluOpType.mult
+ADD = mybir.AluOpType.add
+
+P = 128
+PASSES = K // 512
+WIDE = 512
+REST = T - WIDE
+CHUNK = 256
+
+
+def tile_moe_sup_lin_gelu_kernel(
+    tc, x_words, x_scales, w1_words, w1_scales, w2_words, w2_scales, gate, offs, pos1, pos2, out
+):
+    nc = tc.nc
+    with ExitStack() as ctx:
+        keep = ctx.enter_context(tc.tile_pool(name="keep", bufs=1))
+        psum = ctx.enter_context(tc.psum_pool(name="psum", bufs=1))
+
+        w1s_raw = keep.tile([P, PASSES, H], U8, name="w1s_raw", tag="early_b", align_bytes=64)
+        xs = keep.tile([P, PASSES, T], U8, name="xs", align_bytes=64)
+        nc.vector.memset(w1s_raw[:].bitcast(I32), 0)
+        nc.vector.memset(xs[:].bitcast(I32), 0)
+
+        w1_raw = keep.tile([P, PASSES, 2 * H], U8, name="w1_raw", tag="early_a", align_bytes=64)
+        nc.sync.dma_start(out=w1_raw[:].bitcast(I32), in_=w1_words.rearrange("s p b -> p s b").bitcast(I32))
+        w1s_rows = w1_scales.rearrange("s (q j) i -> j q s i", j=4)
+        for j in range(4):
+            nc.sync.dma_start(out=w1s_raw[j:P:32].bitcast(I32), in_=w1s_rows[j].bitcast(I32))
+        x_rows = x_words.rearrange("s p t d -> p s (t d)")
+        xw = [keep.tile([P, 2, T], U32, name="xw%d" % g, align_bytes=64) for g in range(2)]
+        xs_rows = x_scales.rearrange("s (q j) t -> j q s t", j=4)
+        nc.sync.dma_start(out=xw[0][:].bitcast(I32), in_=x_rows[:, 0:2, :].bitcast(I32))
+        for j in range(4):
+            nc.sync.dma_start(out=xs[j:P:32].bitcast(I32), in_=xs_rows[j].bitcast(I32))
+        nc.sync.dma_start(out=xw[1][:].bitcast(I32), in_=x_rows[:, 2:4, :].bitcast(I32))
+        offs_sb = keep.tile([P, S // 16], U16, name="offs_sb")
+        nc.sync.dma_start(offs_sb[:], offs)
+
+        w1w = {}
+        w1s = {}
+        for u in range(2):
+            sc = keep.tile([P, PASSES, 2, P], U8, name="w1s%d" % u, align_bytes=64)
+            nc.vector.tensor_copy(
+                out=sc[:], in_=w1s_raw[:].rearrange("p s (m r) -> p s r m", r=4)[:, :, 2 * u : 2 * u + 2, :]
+            )
+            w1s[u] = sc
+            for g in range(2):
+                wd = keep.tile([P, 2, 2 * 2 * P], U8, name="w1w%d%d" % (u, g), align_bytes=64)
+                nc.vector.tensor_copy(
+                    out=wd[:].bitcast(U16).rearrange("p s (r m) -> p s r m", r=2),
+                    in_=w1_raw[:, 2 * g : 2 * g + 2, :]
+                    .bitcast(U16)
+                    .rearrange("p s (m r) -> p s r m", r=4)[:, :, 2 * u : 2 * u + 2, :],
+                )
+                w1w[(u, g)] = wd
+
+        w2s = keep.tile([P, E, N], U8, name="w2s", align_bytes=64)
+        nc.vector.memset(w2s[:].bitcast(I32), 0)
+        w2w = keep.tile([P, E, N], U32, name="w2w", tag="early_a", align_bytes=64)
+        nc.sync.dma_start(
+            out=w2w[:].bitcast(I32), in_=w2_words.rearrange("e s p n d -> p (e s) (n d)").bitcast(I32)
+        )
+        w2s_rows = w2_scales.rearrange("e s (q j) n -> j q (e s) n", j=4)
+        for j in range(4):
+            nc.sync.dma_start(out=w2s[j:P:32].bitcast(I32), in_=w2s_rows[j].bitcast(I32))
+        gate_sb = keep.tile([P, 2, T], F32, name="gate_sb", tag="early_b", align_bytes=64)
+        nc.sync.dma_start(out=gate_sb[:], in_=gate.rearrange("r p t -> p r t"))
+        pos_sb = []
+        for name, pos in (("pos1_sb", pos1), ("pos2_sb", pos2)):
+            lst = keep.tile([P, T // 16], U16, name=name)
+            nc.sync.dma_start(lst[:], pos)
+            pos_sb.append(lst)
+
+        def first(acc, u, e, s, cols):
+            nc.tensor.matmul_mx(
+                out=acc,
+                lhsT=w1w[(u, s // 2)][:, s % 2, e * 2 * P : (e + 1) * 2 * P].bitcast(FP4X4),
+                lhsT_scale=w1s[u][:, s, e, :],
+                rhs=xw[s // 2][:, s % 2, cols].bitcast(FP8X4),
+                rhs_scale=xs[:, s, cols],
+                start=(s == 0),
+                stop=(s == PASSES - 1),
+            )
+
+        pairs = []
+        for u in range(2):
+            wide = [psum.tile([P, WIDE], F32, name="wide%d%d" % (u, e), tag="bank%d" % (3 * u + e)) for e in range(2)]
+            rest = psum.tile([P, 2, REST], F32, name="rest%d" % u, tag="bank%d" % (3 * u + 2))
+            for s in range(PASSES):
+                for e in range(2):
+                    first(wide[e][:], u, e, s, slice(0, WIDE))
+            for e in range(2):
+                for s in range(PASSES):
+                    first(rest[:, e, :], u, e, s, slice(WIDE, T))
+            pair = keep.tile([P, T, 2], BF16, name="pair%d" % u, align_bytes=64)
+            for e in range(2):
+                nc.scalar.activation(out=pair[:, 0:WIDE, e], in_=wide[e][:], func=GELU)
+            nc.scalar.activation(out=pair[:, WIDE:T, :], in_=rest[:].rearrange("p e t -> p t e"), func=GELU)
+            pairs.append(pair[:].rearrange("p t e -> p (t e)").bitcast(U32))
+
+        chunks = S // CHUNK
+        cols16 = CHUNK // 16
+        got = [keep.tile([P, 2, CHUNK], U32, name="got%d" % c, align_bytes=64) for c in range(chunks)]
+
+        def gather(u, c):
+            nc.vector.tensor_copy(
+                out=got[c][:, u, :], in_=pairs[u].indirect(offs_sb[:, c * cols16 : (c + 1) * cols16])
+            )
+
+        y = [keep.tile([P, S], F32, name="y%d" % b) for b in range(2)]
+        banks = {}
+
+        def second(c):
+            woven = keep.tile([P, CHUNK, 2], U32, name="woven%d" % c, align_bytes=64)
+            nc.scalar.copy(out=woven[:], in_=got[c][:].rearrange("p u j -> p j u"))
+            codes = keep.tile([P, CHUNK], U32, name="codes%d" % c, align_bytes=64)
+            scales = keep.tile([P, CHUNK], U8, name="scales%d" % c, align_bytes=64)
+            nc.vector.quantize_mx(
+                out=codes[:].bitcast(FP8X4), scales=scales[:], in_=woven[:].rearrange("p j u -> p (j u)").bitcast(BF16)
+            )
+            acc = psum.tile([P, 2, CHUNK], F32, name="acc%d" % c, tag="bank%d" % ((6 + c) % 8))
+            for b in range(2):
+                for k in range(CHUNK // C):
+                    e = c * (CHUNK // C) + k
+                    nc.tensor.matmul_mx(
+                        out=acc[:, b, k * C : (k + 1) * C],
+                        lhsT=w2w[:, e, b * P : (b + 1) * P].bitcast(FP8X4),
+                        lhsT_scale=w2s[:, e, b * P : (b + 1) * P],
+                        rhs=codes[:, k * C : (k + 1) * C].bitcast(FP8X4),
+                        rhs_scale=scales[:, k * C : (k + 1) * C],
+                        start=True,
+                        stop=True,
+                    )
+            banks[c] = acc
+
+        def empty(b, c):
+            nc.scalar.copy(out=y[b][:, c * CHUNK : (c + 1) * CHUNK], in_=banks[c][:, b, :])
+
+        for c in range(chunks):
+            gather(0, c)
+        for c in range(chunks + 2):
+            if c < chunks:
+                gather(1, c)
+            if 1 <= c <= chunks:
+                second(c - 1)
+            if c >= 2:
+                empty(0, c - 2)
+        for c in range(chunks):
+            empty(1, c)
+
+        for b, cuts in ((0, ((0, T),)), (1, ((0, 384), (384, T)))):
+            for lo, hi in cuts:
+                parts = []
+                for r in range(2):
+                    part = keep.tile([P, hi - lo], F32, name="part%d%d%d" % (b, lo, r))
+                    nc.vector.tensor_tensor(
+                        part[:], y[b][:].indirect(pos_sb[r][:, lo // 16 : hi // 16]), gate_sb[:, r, lo:hi], MULT
+                    )
+                    parts.append(part)
+                total = keep.tile([P, hi - lo], F32, name="total%d%d" % (b, lo))
+                nc.vector.tensor_tensor(total[:], parts[0][:], parts[1][:], ADD)
+                nc.sync.dma_start(out=out[b * P : (b + 1) * P, lo:hi], in_=total[:])

@@ -1,6 +1,7 @@
 from contextlib import ExitStack
 
 import concourse.mybir as mybir
+from concourse.masks import make_identity
 
 K, T, E, C, H, N = 2048, 640, 10, 128, 512, 256
 S = E * C
@@ -20,9 +21,14 @@ ADD = mybir.AluOpType.add
 
 P = 128
 PASSES = K // 512
-WIDE = 512
-REST = T - WIDE
-CHUNK = 256
+BANK = 512
+LIST = 16
+
+X_LOADS = ((0, 256), (256, 384), (384, 512), (512, 640))
+GATHERS = ((448, 448, 384), (256, 256, 256, 256, 256))
+CHUNKS = (256, 256, 256, 256, 128, 128)
+CHUNKS_BY_SCALAR = 4
+PIECES = ((0, 0, 384), (0, 384, 640), (1, 0, 512), (1, 512, 640))
 
 
 def tile_moe_sup_lin_gelu_kernel(
@@ -33,147 +39,189 @@ def tile_moe_sup_lin_gelu_kernel(
         keep = ctx.enter_context(tc.tile_pool(name="keep", bufs=1))
         psum = ctx.enter_context(tc.psum_pool(name="psum", bufs=1))
 
-        w1s_raw = keep.tile([P, PASSES, H], U8, name="w1s_raw", tag="early_b", align_bytes=64)
-        xs = keep.tile([P, PASSES, T], U8, name="xs", align_bytes=64)
-        nc.vector.memset(w1s_raw[:].bitcast(I32), 0)
-        nc.vector.memset(xs[:].bitcast(I32), 0)
+        def bank_tile(shape, name, bank):
+            return psum.tile(shape, F32, name=name, tag="bank%d" % bank)
 
-        w1_raw = keep.tile([P, PASSES, 2 * H], U8, name="w1_raw", tag="early_a", align_bytes=64)
+        def load_scale_rows(plane, rows):
+            for j in range(4):
+                nc.sync.dma_start(out=plane[j:P:32].bitcast(I32), in_=rows[j].bitcast(I32))
+
+        w1_scales_raw = keep.tile([P, PASSES, H], U8, name="w1_scales_raw", align_bytes=64)
+        x_scales_sb = keep.tile([P, PASSES, T], U8, name="x_scales_sb", align_bytes=64)
+        nc.vector.memset(w1_scales_raw[:].bitcast(I32), 0)
+        nc.vector.memset(x_scales_sb[:].bitcast(I32), 0)
+
+        w1_raw = keep.tile([P, PASSES, 2 * H], U8, name="w1_raw", tag="w1_raw", align_bytes=64)
         nc.sync.dma_start(out=w1_raw[:].bitcast(I32), in_=w1_words.rearrange("s p b -> p s b").bitcast(I32))
-        w1s_rows = w1_scales.rearrange("s (q j) i -> j q s i", j=4)
-        for j in range(4):
-            nc.sync.dma_start(out=w1s_raw[j:P:32].bitcast(I32), in_=w1s_rows[j].bitcast(I32))
-        x_rows = x_words.rearrange("s p t d -> p s (t d)")
-        xw = [keep.tile([P, 2, T], U32, name="xw%d" % g, align_bytes=64) for g in range(2)]
-        xs_rows = x_scales.rearrange("s (q j) t -> j q s t", j=4)
-        nc.sync.dma_start(out=xw[0][:].bitcast(I32), in_=x_rows[:, 0:2, :].bitcast(I32))
-        for j in range(4):
-            nc.sync.dma_start(out=xs[j:P:32].bitcast(I32), in_=xs_rows[j].bitcast(I32))
-        nc.sync.dma_start(out=xw[1][:].bitcast(I32), in_=x_rows[:, 2:4, :].bitcast(I32))
-        offs_sb = keep.tile([P, S // 16], U16, name="offs_sb")
+        load_scale_rows(w1_scales_raw, w1_scales.rearrange("s (q j) i -> j q s i", j=4))
+        x_rows = x_words.rearrange("s p t d -> p s (t d)").bitcast(I32)
+        x_sb = keep.tile([P, PASSES, T], U32, name="x_sb", align_bytes=64)
+        for lo, hi in X_LOADS:
+            nc.sync.dma_start(out=x_sb[:, :, lo:hi].bitcast(I32), in_=x_rows[:, :, lo:hi])
+            if lo == 0:
+                load_scale_rows(x_scales_sb, x_scales.rearrange("s (q j) t -> j q s t", j=4))
+        offs_sb = keep.tile([P, S // LIST], U16, name="offs_sb")
         nc.sync.dma_start(offs_sb[:], offs)
 
-        w1w = {}
-        w1s = {}
-        for u in range(2):
-            sc = keep.tile([P, PASSES, 2, P], U8, name="w1s%d" % u, align_bytes=64)
-            nc.vector.tensor_copy(
-                out=sc[:], in_=w1s_raw[:].rearrange("p s (m r) -> p s r m", r=4)[:, :, 2 * u : 2 * u + 2, :]
-            )
-            w1s[u] = sc
-            for g in range(2):
-                wd = keep.tile([P, 2, 2 * 2 * P], U8, name="w1w%d%d" % (u, g), align_bytes=64)
-                nc.vector.tensor_copy(
-                    out=wd[:].bitcast(U16).rearrange("p s (r m) -> p s r m", r=2),
-                    in_=w1_raw[:, 2 * g : 2 * g + 2, :]
-                    .bitcast(U16)
-                    .rearrange("p s (m r) -> p s r m", r=4)[:, :, 2 * u : 2 * u + 2, :],
-                )
-                w1w[(u, g)] = wd
+        w1_grouped = {}
+        w1_scales_grouped = {}
 
-        w2s = keep.tile([P, E, N], U8, name="w2s", align_bytes=64)
-        nc.vector.memset(w2s[:].bitcast(I32), 0)
-        w2w = keep.tile([P, E, N], U32, name="w2w", tag="early_a", align_bytes=64)
-        nc.sync.dma_start(
-            out=w2w[:].bitcast(I32), in_=w2_words.rearrange("e s p n d -> p (e s) (n d)").bitcast(I32)
-        )
-        w2s_rows = w2_scales.rearrange("e s (q j) n -> j q (e s) n", j=4)
-        for j in range(4):
-            nc.sync.dma_start(out=w2s[j:P:32].bitcast(I32), in_=w2s_rows[j].bitcast(I32))
-        gate_sb = keep.tile([P, 2, T], F32, name="gate_sb", tag="early_b", align_bytes=64)
-        nc.sync.dma_start(out=gate_sb[:], in_=gate.rearrange("r p t -> p r t"))
+        def regroup_scales(u):
+            grouped = keep.tile([P, PASSES, 2, P], U8, name="w1_scales%d" % u, align_bytes=64)
+            nc.vector.tensor_copy(
+                out=grouped[:],
+                in_=w1_scales_raw[:].rearrange("p s (m d) -> p s d m", d=4)[:, :, 2 * u : 2 * u + 2, :],
+            )
+            w1_scales_grouped[u] = grouped
+
+        def regroup_words(u, half):
+            grouped = keep.tile([P, 2, 2 * 2 * P], U8, name="w1_words%d%d" % (u, half), align_bytes=64)
+            source = w1_raw[:, 2 * half : 2 * half + 2, :].bitcast(U16).rearrange("p s (m d) -> p s d m", d=4)
+            nc.vector.tensor_copy(
+                out=grouped[:].bitcast(U16).rearrange("p s (e m) -> p s e m", e=2),
+                in_=source[:, :, 2 * u : 2 * u + 2, :],
+            )
+            w1_grouped[(u, half)] = grouped
+
+        regroup_words(0, 0)
+        regroup_scales(0)
+        regroup_words(0, 1)
+        regroup_scales(1)
+        regroup_words(1, 0)
+        regroup_words(1, 1)
+
+        w2_scales_sb = keep.tile([P, E, N], U8, name="w2_scales_sb", align_bytes=64)
+        nc.vector.memset(w2_scales_sb[:].bitcast(I32), 0)
+        w2_sb = keep.tile([P, E, N], U32, name="w2_sb", align_bytes=64)
+        nc.sync.dma_start(out=w2_sb[:].bitcast(I32), in_=w2_words.rearrange("e s p n d -> p (e s) (n d)").bitcast(I32))
+        load_scale_rows(w2_scales_sb, w2_scales.rearrange("e s (q j) n -> j q (e s) n", j=4))
         pos_sb = []
         for name, pos in (("pos1_sb", pos1), ("pos2_sb", pos2)):
-            lst = keep.tile([P, T // 16], U16, name=name)
-            nc.sync.dma_start(lst[:], pos)
-            pos_sb.append(lst)
+            pos_tile = keep.tile([P, T // LIST], U16, name=name)
+            nc.sync.dma_start(pos_tile[:], pos)
+            pos_sb.append(pos_tile)
+        gate_sb = keep.tile([P, 2, T], F32, name="gate_sb")
+        nc.sync.dma_start(out=gate_sb[:], in_=gate.rearrange("r p t -> p r t"))
 
-        def first(acc, u, e, s, cols):
-            nc.tensor.matmul_mx(
-                out=acc,
-                lhsT=w1w[(u, s // 2)][:, s % 2, e * 2 * P : (e + 1) * 2 * P].bitcast(FP4X4),
-                lhsT_scale=w1s[u][:, s, e, :],
-                rhs=xw[s // 2][:, s % 2, cols].bitcast(FP8X4),
-                rhs_scale=xs[:, s, cols],
-                start=(s == 0),
-                stop=(s == PASSES - 1),
-            )
-
-        pairs = []
-        for u in range(2):
-            wide = [psum.tile([P, WIDE], F32, name="wide%d%d" % (u, e), tag="bank%d" % (3 * u + e)) for e in range(2)]
-            rest = psum.tile([P, 2, REST], F32, name="rest%d" % u, tag="bank%d" % (3 * u + 2))
+        def first_layer(acc, u, e, lo, hi):
             for s in range(PASSES):
-                for e in range(2):
-                    first(wide[e][:], u, e, s, slice(0, WIDE))
-            for e in range(2):
-                for s in range(PASSES):
-                    first(rest[:, e, :], u, e, s, slice(WIDE, T))
-            pair = keep.tile([P, T, 2], BF16, name="pair%d" % u, align_bytes=64)
-            for e in range(2):
-                nc.scalar.activation(out=pair[:, 0:WIDE, e], in_=wide[e][:], func=GELU)
-            nc.scalar.activation(out=pair[:, WIDE:T, :], in_=rest[:].rearrange("p e t -> p t e"), func=GELU)
-            pairs.append(pair[:].rearrange("p t e -> p (t e)").bitcast(U32))
+                nc.tensor.matmul_mx(
+                    out=acc,
+                    lhsT=w1_grouped[(u, s // 2)][:, s % 2, e * 2 * P : (e + 1) * 2 * P].bitcast(FP4X4),
+                    lhsT_scale=w1_scales_grouped[u][:, s, e, :],
+                    rhs=x_sb[:, s, lo:hi].bitcast(FP8X4),
+                    rhs_scale=x_scales_sb[:, s, lo:hi],
+                    start=(s == 0),
+                    stop=(s == PASSES - 1),
+                )
 
-        chunks = S // CHUNK
-        cols16 = CHUNK // 16
-        got = [keep.tile([P, 2, CHUNK], U32, name="got%d" % c, align_bytes=64) for c in range(chunks)]
+        def token_tile(u, lo, bank):
+            acc = bank_tile([P, 2, P], "hidden%d_%d" % (u, lo), bank)
+            for e in range(2):
+                first_layer(acc[:, e, :], u, e, lo, lo + P)
+            nc.scalar.activation(out=pairs[u][:, lo : lo + P, :], in_=acc[:].rearrange("p e t -> p t e"), func=GELU)
 
-        def gather(u, c):
-            nc.vector.tensor_copy(
-                out=got[c][:, u, :], in_=pairs[u].indirect(offs_sb[:, c * cols16 : (c + 1) * cols16])
-            )
+        identity = keep.tile([P, P], F32, name="identity", tag="w1_raw", align_bytes=64)
+        make_identity(nc, identity[:])
+        pairs = [keep.tile([P, T, 2], BF16, name="pair%d" % u, align_bytes=64) for u in range(2)]
+        for lo in range(0, T, P):
+            token_tile(0, lo, lo // P)
+        for e in range(2):
+            wide = bank_tile([P, BANK], "wide%d" % e, 3 + e)
+            first_layer(wide[:], 1, e, 0, BANK)
+            nc.scalar.activation(out=pairs[1][:, 0:BANK, e], in_=wide[:], func=GELU)
+        token_tile(1, BANK, 3)
+
+        gathered = keep.tile([P, 2 * S], U32, name="gathered", align_bytes=64)
+        for u, widths in enumerate(GATHERS):
+            window = pairs[u][:].rearrange("p t e -> p (t e)").bitcast(U32)
+            lo = 0
+            for width in widths:
+                nc.vector.tensor_copy(
+                    out=gathered[:, u * S + lo : u * S + lo + width],
+                    in_=window.indirect(offs_sb[:, lo // LIST : (lo + width) // LIST]),
+                )
+                lo = lo + width
 
         y = [keep.tile([P, S], F32, name="y%d" % b) for b in range(2)]
-        banks = {}
+        starts = [sum(CHUNKS[:c]) for c in range(len(CHUNKS) + 1)]
+        quantised = []
 
-        def second(c):
-            woven = keep.tile([P, CHUNK, 2], U32, name="woven%d" % c, align_bytes=64)
-            nc.scalar.copy(out=woven[:], in_=got[c][:].rearrange("p u j -> p j u"))
-            codes = keep.tile([P, CHUNK], U32, name="codes%d" % c, align_bytes=64)
-            scales = keep.tile([P, CHUNK], U8, name="scales%d" % c, align_bytes=64)
-            nc.vector.quantize_mx(
-                out=codes[:].bitcast(FP8X4), scales=scales[:], in_=woven[:].rearrange("p j u -> p (j u)").bitcast(BF16)
+        def expert(acc, b, c, at):
+            codes, scales = quantised[c]
+            which = (starts[c] + at) // C
+            nc.tensor.matmul_mx(
+                out=acc,
+                lhsT=w2_sb[:, which, b * P : (b + 1) * P].bitcast(FP8X4),
+                lhsT_scale=w2_scales_sb[:, which, b * P : (b + 1) * P],
+                rhs=codes[:, at : at + C].bitcast(FP8X4),
+                rhs_scale=scales[:, at : at + C],
+                start=True,
+                stop=True,
             )
-            acc = psum.tile([P, 2, CHUNK], F32, name="acc%d" % c, tag="bank%d" % ((6 + c) % 8))
-            for b in range(2):
-                for k in range(CHUNK // C):
-                    e = c * (CHUNK // C) + k
-                    nc.tensor.matmul_mx(
-                        out=acc[:, b, k * C : (k + 1) * C],
-                        lhsT=w2w[:, e, b * P : (b + 1) * P].bitcast(FP8X4),
-                        lhsT_scale=w2s[:, e, b * P : (b + 1) * P],
-                        rhs=codes[:, k * C : (k + 1) * C].bitcast(FP8X4),
-                        rhs_scale=scales[:, k * C : (k + 1) * C],
-                        start=True,
-                        stop=True,
-                    )
-            banks[c] = acc
 
-        def empty(b, c):
-            nc.scalar.copy(out=y[b][:, c * CHUNK : (c + 1) * CHUNK], in_=banks[c][:, b, :])
+        block0_banks = (5, 6, 0, 1, 2, 3)
+        block0 = []
+        for c, width in enumerate(CHUNKS):
+            woven = keep.tile([P, width, 2], U32, name="woven%d" % c, align_bytes=64)
+            nc.scalar.copy(
+                out=woven[:], in_=gathered[:].rearrange("p (u j) -> p j u", u=2)[:, starts[c] : starts[c + 1], :]
+            )
+            codes = keep.tile([P, width], U32, name="codes%d" % c, align_bytes=64)
+            scales = keep.tile([P, width], U8, name="scales%d" % c, align_bytes=64)
+            nc.vector.quantize_mx(
+                out=codes[:].bitcast(FP8X4),
+                scales=scales[:],
+                in_=woven[:].rearrange("p j u -> p (j u)").bitcast(BF16),
+            )
+            quantised.append((codes, scales))
+            acc = bank_tile([P, width], "block0_%d" % c, block0_banks[c])
+            for at in range(0, width, C):
+                expert(acc[:, at : at + C], 0, c, at)
+            block0.append(acc)
+        for c, acc in enumerate(block0):
+            empty = nc.scalar.copy if c < CHUNKS_BY_SCALAR else nc.vector.tensor_copy
+            empty(out=y[0][:, starts[c] : starts[c + 1]], in_=acc[:])
 
-        for c in range(chunks):
-            gather(0, c)
-        for c in range(chunks + 2):
-            if c < chunks:
-                gather(1, c)
-            if 1 <= c <= chunks:
-                second(c - 1)
-            if c >= 2:
-                empty(0, c - 2)
-        for c in range(chunks):
-            empty(1, c)
+        block1 = [
+            bank_tile([P, min(BANK, S - lo)], "block1_%d" % lo, bank)
+            for lo, bank in zip(range(0, S, BANK), block0_banks[-3:])
+        ]
+        for c, width in enumerate(CHUNKS):
+            for at in range(0, width, C):
+                slot = starts[c] + at
+                expert(block1[slot // BANK][:, slot % BANK : slot % BANK + C], 1, c, at)
+        for k, acc in enumerate(block1):
+            nc.scalar.copy(out=y[1][:, k * BANK : min((k + 1) * BANK, S)], in_=acc[:])
 
-        for b, cuts in ((0, ((0, T),)), (1, ((0, 384), (384, T)))):
-            for lo, hi in cuts:
-                parts = []
-                for r in range(2):
-                    part = keep.tile([P, hi - lo], F32, name="part%d%d%d" % (b, lo, r))
-                    nc.vector.tensor_tensor(
-                        part[:], y[b][:].indirect(pos_sb[r][:, lo // 16 : hi // 16]), gate_sb[:, r, lo:hi], MULT
-                    )
-                    parts.append(part)
-                total = keep.tile([P, hi - lo], F32, name="total%d%d" % (b, lo))
-                nc.vector.tensor_tensor(total[:], parts[0][:], parts[1][:], ADD)
-                nc.sync.dma_start(out=out[b * P : (b + 1) * P, lo:hi], in_=total[:])
+        for n, (b, lo, hi) in enumerate(PIECES):
+            products = []
+            for r in range(2):
+                product = keep.tile([P, hi - lo], F32, name="product%d%d" % (n, r))
+                picked = y[b][:].indirect(pos_sb[r][:, lo // LIST : hi // LIST])
+                nc.vector.tensor_tensor(product[:], picked, gate_sb[:, r, lo:hi], MULT)
+                products.append(product)
+            total = keep.tile([P, hi - lo], F32, name="total%d" % n)
+            rows = out[b * P : (b + 1) * P, lo:hi]
+            if b == 0:
+                turned_sum = bank_tile([P, hi - lo], "turned_sum%d" % n, block0_banks[-1 - n])
+                for at in range(0, hi - lo, P):
+                    for r in range(2):
+                        nc.tensor.matmul(
+                            turned_sum[:, at : at + P],
+                            lhsT=products[r][:, at : at + P],
+                            rhs=identity[:],
+                            is_transpose=True,
+                            start=(r == 0),
+                            stop=(r == 1),
+                        )
+                turned = keep.tile([P, hi - lo], F32, name="turned%d" % n)
+                nc.scalar.copy(out=turned[:], in_=turned_sum[:])
+                turned_back = bank_tile([P, hi - lo], "turned_back%d" % n, 4 + n)
+                for at in range(0, hi - lo, P):
+                    nc.tensor.transpose(turned_back[:, at : at + P], turned[:, at : at + P], identity[:])
+                nc.scalar.copy(out=total[:], in_=turned_back[:])
+                nc.scalar.dma_start(out=rows, in_=total[:])
+            else:
+                nc.vector.tensor_tensor(total[:], products[0][:], products[1][:], ADD)
+                nc.sync.dma_start(out=rows, in_=total[:])

@@ -24,7 +24,6 @@ PASSES = K // 512
 BANK = 512
 LIST = 16
 
-X_LOADS = ((0, 256), (256, 384), (384, 512), (512, 640))
 GATHERS = ((448, 448, 384), (256, 256, 256, 256, 256))
 CHUNKS = (256, 256, 256, 256, 128, 128)
 CHUNKS_BY_SCALAR = 4
@@ -51,17 +50,33 @@ def tile_moe_sup_lin_gelu_kernel(
         nc.vector.memset(w1_scales_raw[:].bitcast(I32), 0)
         nc.vector.memset(x_scales_sb[:].bitcast(I32), 0)
 
-        w1_raw = keep.tile([P, PASSES, 2 * H], U8, name="w1_raw", tag="w1_raw", align_bytes=64)
-        nc.sync.dma_start(out=w1_raw[:].bitcast(I32), in_=w1_words.rearrange("s p b -> p s b").bitcast(I32))
-        load_scale_rows(w1_scales_raw, w1_scales.rearrange("s (q j) i -> j q s i", j=4))
-        x_rows = x_words.rearrange("s p t d -> p s (t d)").bitcast(I32)
-        x_sb = keep.tile([P, PASSES, T], U32, name="x_sb", align_bytes=64)
-        for lo, hi in X_LOADS:
-            nc.sync.dma_start(out=x_sb[:, :, lo:hi].bitcast(I32), in_=x_rows[:, :, lo:hi])
-            if lo == 0:
-                load_scale_rows(x_scales_sb, x_scales.rearrange("s (q j) t -> j q s t", j=4))
         offs_sb = keep.tile([P, S // LIST], U16, name="offs_sb")
         nc.sync.dma_start(offs_sb[:], offs)
+        w1_rows = w1_words.rearrange("s p b -> p s b").bitcast(I32)
+        x_rows = x_words.rearrange("s p t d -> p s (t d)").bitcast(I32)
+        w1_raw = []
+        x_tiles = {}
+
+        def load_w1(half):
+            raw = keep.tile([P, 2, 2 * H], U8, name="w1_raw%d" % half, tag="w1_raw%d" % half, align_bytes=64)
+            nc.sync.dma_start(out=raw[:].bitcast(I32), in_=w1_rows[:, 2 * half : 2 * half + 2, :])
+            w1_raw.append(raw)
+
+        def load_x(s0, s1, lo, hi):
+            part = keep.tile([P, s1 - s0, hi - lo], U32, name="x%d_%d" % (s0, lo), align_bytes=64)
+            nc.sync.dma_start(out=part[:].bitcast(I32), in_=x_rows[:, s0:s1, lo:hi])
+            for s in range(s0, s1):
+                x_tiles[(s, lo)] = part[:, s - s0, :]
+
+        load_x(0, 1, 0, BANK)
+        load_scale_rows(w1_scales_raw, w1_scales.rearrange("s (q j) i -> j q s i", j=4))
+        load_w1(0)
+        load_x(1, 2, 0, BANK)
+        load_scale_rows(x_scales_sb, x_scales.rearrange("s (q j) t -> j q s t", j=4))
+        load_w1(1)
+        load_x(2, 3, 0, BANK)
+        load_x(3, 4, 0, BANK)
+        load_x(0, 4, BANK, T)
 
         w1_grouped = {}
         w1_scales_grouped = {}
@@ -74,63 +89,79 @@ def tile_moe_sup_lin_gelu_kernel(
             )
             w1_scales_grouped[u] = grouped
 
-        def regroup_words(u, half):
-            grouped = keep.tile([P, 2, 2 * 2 * P], U8, name="w1_words%d%d" % (u, half), align_bytes=64)
-            source = w1_raw[:, 2 * half : 2 * half + 2, :].bitcast(U16).rearrange("p s (m d) -> p s d m", d=4)
+        def regroup_words(u, s0, s1):
+            grouped = keep.tile([P, s1 - s0, 2 * 2 * P], U8, name="w1_words%d%d" % (u, s0), align_bytes=64)
+            source = w1_raw[s0 // 2][:, s0 % 2 : s0 % 2 + s1 - s0, :].bitcast(U16).rearrange("p s (m d) -> p s d m", d=4)
             nc.vector.tensor_copy(
                 out=grouped[:].bitcast(U16).rearrange("p s (e m) -> p s e m", e=2),
                 in_=source[:, :, 2 * u : 2 * u + 2, :],
             )
-            w1_grouped[(u, half)] = grouped
+            for s in range(s0, s1):
+                w1_grouped[(u, s)] = grouped[:, s - s0, :]
 
-        regroup_words(0, 0)
         regroup_scales(0)
-        regroup_words(0, 1)
         regroup_scales(1)
-        regroup_words(1, 0)
-        regroup_words(1, 1)
+        regroup_words(0, 0, 1)
+        regroup_words(0, 1, 2)
+        regroup_words(0, 2, 4)
+        regroup_words(1, 0, 2)
+        regroup_words(1, 2, 4)
 
         w2_scales_sb = keep.tile([P, E, N], U8, name="w2_scales_sb", align_bytes=64)
         nc.vector.memset(w2_scales_sb[:].bitcast(I32), 0)
         w2_sb = keep.tile([P, E, N], U32, name="w2_sb", align_bytes=64)
         nc.sync.dma_start(out=w2_sb[:].bitcast(I32), in_=w2_words.rearrange("e s p n d -> p (e s) (n d)").bitcast(I32))
         load_scale_rows(w2_scales_sb, w2_scales.rearrange("e s (q j) n -> j q (e s) n", j=4))
-        pos_sb = []
-        for name, pos in (("pos1_sb", pos1), ("pos2_sb", pos2)):
-            pos_tile = keep.tile([P, T // LIST], U16, name=name)
-            nc.sync.dma_start(pos_tile[:], pos)
-            pos_sb.append(pos_tile)
+        pos_sb = [keep.tile([P, T // LIST], U16, name="pos%d_sb" % (r + 1)) for r in range(2)]
+        nc.sync.dma_start(pos_sb[0][:], pos1)
+        nc.sync.dma_start(pos_sb[1][:], pos2)
         gate_sb = keep.tile([P, 2, T], F32, name="gate_sb")
         nc.sync.dma_start(out=gate_sb[:], in_=gate.rearrange("r p t -> p r t"))
 
-        def first_layer(acc, u, e, lo, hi):
-            for s in range(PASSES):
-                nc.tensor.matmul_mx(
-                    out=acc,
-                    lhsT=w1_grouped[(u, s // 2)][:, s % 2, e * 2 * P : (e + 1) * 2 * P].bitcast(FP4X4),
-                    lhsT_scale=w1_scales_grouped[u][:, s, e, :],
-                    rhs=x_sb[:, s, lo:hi].bitcast(FP8X4),
-                    rhs_scale=x_scales_sb[:, s, lo:hi],
-                    start=(s == 0),
-                    stop=(s == PASSES - 1),
-                )
+        def first_pass(acc, u, e, s, lo, hi, last):
+            nc.tensor.matmul_mx(
+                out=acc,
+                lhsT=w1_grouped[(u, s)][:, e * 2 * P : (e + 1) * 2 * P].bitcast(FP4X4),
+                lhsT_scale=w1_scales_grouped[u][:, s, e, :],
+                rhs=x_tiles[(s, lo)].bitcast(FP8X4),
+                rhs_scale=x_scales_sb[:, s, lo:hi],
+                start=(s == 0),
+                stop=last,
+            )
 
-        def token_tile(u, lo, bank):
-            acc = bank_tile([P, 2, P], "hidden%d_%d" % (u, lo), bank)
+        warm = bank_tile([P, BANK], "warm", 7)
+        for width in (512, 512, 256):
+            nc.tensor.matmul_mx(
+                out=warm[:, 0:width],
+                lhsT=x_tiles[(0, 0)][:, 0:P].bitcast(FP8X4),
+                lhsT_scale=w1_scales_raw[:, 0, 0:P],
+                rhs=x_tiles[(0, 0)][:, 0:width].bitcast(FP8X4),
+                rhs_scale=w1_scales_raw[:, 0, 0:width],
+                start=True,
+                stop=True,
+            )
+
+        def last_tokens(u, bank):
+            acc = bank_tile([P, 2, P], "hidden%d" % u, bank)
             for e in range(2):
-                first_layer(acc[:, e, :], u, e, lo, lo + P)
-            nc.scalar.activation(out=pairs[u][:, lo : lo + P, :], in_=acc[:].rearrange("p e t -> p t e"), func=GELU)
+                for s in range(PASSES):
+                    first_pass(acc[:, e, :], u, e, s, BANK, T, s == PASSES - 1)
+            nc.scalar.activation(out=pairs[u][:, BANK:T, :], in_=acc[:].rearrange("p e t -> p t e"), func=GELU)
 
-        identity = keep.tile([P, P], F32, name="identity", tag="w1_raw", align_bytes=64)
+        identity = keep.tile([P, P], F32, name="identity", tag="w1_raw1", align_bytes=64)
         make_identity(nc, identity[:])
         pairs = [keep.tile([P, T, 2], BF16, name="pair%d" % u, align_bytes=64) for u in range(2)]
-        for lo in range(0, T, P):
-            token_tile(0, lo, lo // P)
-        for e in range(2):
-            wide = bank_tile([P, BANK], "wide%d" % e, 3 + e)
-            first_layer(wide[:], 1, e, 0, BANK)
-            nc.scalar.activation(out=pairs[1][:, 0:BANK, e], in_=wide[:], func=GELU)
-        token_tile(1, BANK, 3)
+        for u, banks in enumerate(((0, 1, 2), (0, 1, 2))):
+            wide = [bank_tile([P, BANK], "wide%d%d" % (u, e), banks[e]) for e in range(2)]
+            order = [(0, 0), (1, 0), (0, 1), (0, 2), (0, 3), (1, 3), (1, 2), (1, 1)]
+            if u == 1:
+                order = sorted(order, key=lambda step: step[0])
+            for n, (e, s) in enumerate(order):
+                last = (e, s) in ((0, 3), (1, 1))
+                first_pass(wide[e][:], u, e, s, 0, BANK, last)
+                if last:
+                    nc.scalar.activation(out=pairs[u][:, 0:BANK, e], in_=wide[e][:], func=GELU)
+            last_tokens(u, banks[2])
 
         gathered = keep.tile([P, 2 * S], U32, name="gathered", align_bytes=64)
         for u, widths in enumerate(GATHERS):

@@ -27,7 +27,8 @@ LIST = 16
 GATHERS = ((448, 448, 384), (256, 256, 256, 256, 256))
 CHUNKS = (256, 256, 256, 256, 128, 128)
 CHUNKS_BY_SCALAR = 4
-PIECES = ((0, 0, 384), (0, 384, 640), (1, 0, 512), (1, 512, 640))
+BLOCK0_PIECES = ((0, 384), (384, 640))
+BLOCK1_CUTS = (320, 448)
 
 
 def tile_moe_sup_lin_gelu_kernel(
@@ -225,34 +226,50 @@ def tile_moe_sup_lin_gelu_kernel(
         for k, acc in enumerate(block1):
             nc.scalar.copy(out=y[1][:, k * BANK : min((k + 1) * BANK, S)], in_=acc[:])
 
-        for n, (b, lo, hi) in enumerate(PIECES):
-            products = []
+        def product_tiles(name, width):
+            return [keep.tile([P, width], F32, name="%s%d" % (name, r)) for r in range(2)]
+
+        def gather_product(product, b, r, lo, hi):
+            picked = y[b][:].indirect(pos_sb[r][:, lo // LIST : hi // LIST])
+            nc.vector.tensor_tensor(product[:], picked, gate_sb[:, r, lo:hi], MULT)
+
+        for n, (lo, hi) in enumerate(BLOCK0_PIECES):
+            products = product_tiles("product0_%d_" % n, hi - lo)
             for r in range(2):
-                product = keep.tile([P, hi - lo], F32, name="product%d%d" % (n, r))
-                picked = y[b][:].indirect(pos_sb[r][:, lo // LIST : hi // LIST])
-                nc.vector.tensor_tensor(product[:], picked, gate_sb[:, r, lo:hi], MULT)
-                products.append(product)
+                gather_product(products[r], 0, r, lo, hi)
+            turned_sum = bank_tile([P, hi - lo], "turned_sum%d" % n, block0_banks[-1 - n])
+            for at in range(0, hi - lo, P):
+                for r in range(2):
+                    nc.tensor.matmul(
+                        turned_sum[:, at : at + P],
+                        lhsT=products[r][:, at : at + P],
+                        rhs=identity[:],
+                        is_transpose=True,
+                        start=(r == 0),
+                        stop=(r == 1),
+                    )
+            turned = keep.tile([P, hi - lo], F32, name="turned%d" % n)
+            nc.scalar.copy(out=turned[:], in_=turned_sum[:])
+            turned_back = bank_tile([P, hi - lo], "turned_back%d" % n, 4 + n)
+            for at in range(0, hi - lo, P):
+                nc.tensor.transpose(turned_back[:, at : at + P], turned[:, at : at + P], identity[:])
             total = keep.tile([P, hi - lo], F32, name="total%d" % n)
-            rows = out[b * P : (b + 1) * P, lo:hi]
-            if b == 0:
-                turned_sum = bank_tile([P, hi - lo], "turned_sum%d" % n, block0_banks[-1 - n])
-                for at in range(0, hi - lo, P):
-                    for r in range(2):
-                        nc.tensor.matmul(
-                            turned_sum[:, at : at + P],
-                            lhsT=products[r][:, at : at + P],
-                            rhs=identity[:],
-                            is_transpose=True,
-                            start=(r == 0),
-                            stop=(r == 1),
-                        )
-                turned = keep.tile([P, hi - lo], F32, name="turned%d" % n)
-                nc.scalar.copy(out=turned[:], in_=turned_sum[:])
-                turned_back = bank_tile([P, hi - lo], "turned_back%d" % n, 4 + n)
-                for at in range(0, hi - lo, P):
-                    nc.tensor.transpose(turned_back[:, at : at + P], turned[:, at : at + P], identity[:])
-                nc.scalar.copy(out=total[:], in_=turned_back[:])
-                nc.scalar.dma_start(out=rows, in_=total[:])
-            else:
-                nc.vector.tensor_tensor(total[:], products[0][:], products[1][:], ADD)
-                nc.sync.dma_start(out=rows, in_=total[:])
+            nc.scalar.copy(out=total[:], in_=turned_back[:])
+            nc.scalar.dma_start(out=out[0:P, lo:hi], in_=total[:])
+
+        def add_and_store(products, at, lo, hi):
+            total = keep.tile([P, hi - lo], F32, name="total1_%d" % lo)
+            cols = slice(at, at + hi - lo)
+            nc.vector.tensor_tensor(total[:], products[0][:, cols], products[1][:, cols], ADD)
+            nc.sync.dma_start(out=out[P : 2 * P, lo:hi], in_=total[:])
+
+        early_sum, first_gather = BLOCK1_CUTS
+        head = product_tiles("head", first_gather)
+        tail = product_tiles("tail", T - first_gather)
+        for r in range(2):
+            gather_product(head[r], 1, r, 0, first_gather)
+        gather_product(tail[0], 1, 0, first_gather, T)
+        add_and_store(head, 0, 0, early_sum)
+        gather_product(tail[1], 1, 1, first_gather, T)
+        add_and_store(head, early_sum, early_sum, first_gather)
+        add_and_store(tail, 0, first_gather, T)

@@ -28,7 +28,10 @@ GATHERS = ((448, 448, 384), (256, 256, 256, 256, 256))
 CHUNKS = (256, 256, 256, 256, 128, 128)
 CHUNKS_BY_SCALAR = 4
 BLOCK0_PIECES = ((0, 384), (384, 640))
-BLOCK1_CUTS = (320, 448)
+HEAD_TOKENS = 448
+EARLY_SUMS = 320
+PAIR0_ORDER = ((0, 0), (1, 0), (0, 1), (0, 2), (0, 3), (1, 3), (1, 2), (1, 1))
+WARM_UP = (512, 512, 256)
 
 
 def tile_moe_sup_lin_gelu_kernel(
@@ -51,8 +54,6 @@ def tile_moe_sup_lin_gelu_kernel(
         nc.vector.memset(w1_scales_raw[:].bitcast(I32), 0)
         nc.vector.memset(x_scales_sb[:].bitcast(I32), 0)
 
-        offs_sb = keep.tile([P, S // LIST], U16, name="offs_sb")
-        nc.sync.dma_start(offs_sb[:], offs)
         w1_rows = w1_words.rearrange("s p b -> p s b").bitcast(I32)
         x_rows = x_words.rearrange("s p t d -> p s (t d)").bitcast(I32)
         w1_raw = []
@@ -70,6 +71,8 @@ def tile_moe_sup_lin_gelu_kernel(
                 x_tiles[(s, lo)] = part[:, s - s0, :]
 
         load_x(0, 1, 0, BANK)
+        offs_sb = keep.tile([P, S // LIST], U16, name="offs_sb")
+        nc.sync.dma_start(offs_sb[:], offs)
         load_scale_rows(w1_scales_raw, w1_scales.rearrange("s (q j) i -> j q s i", j=4))
         load_w1(0)
         load_x(1, 2, 0, BANK)
@@ -77,7 +80,7 @@ def tile_moe_sup_lin_gelu_kernel(
         load_w1(1)
         load_x(2, 3, 0, BANK)
         load_x(3, 4, 0, BANK)
-        load_x(0, 4, BANK, T)
+        load_x(0, PASSES, BANK, T)
 
         w1_grouped = {}
         w1_scales_grouped = {}
@@ -131,7 +134,7 @@ def tile_moe_sup_lin_gelu_kernel(
             )
 
         warm = bank_tile([P, BANK], "warm", 7)
-        for width in (512, 512, 256):
+        for width in WARM_UP:
             nc.tensor.matmul_mx(
                 out=warm[:, 0:width],
                 lhsT=x_tiles[(0, 0)][:, 0:P].bitcast(FP8X4),
@@ -152,17 +155,14 @@ def tile_moe_sup_lin_gelu_kernel(
         identity = keep.tile([P, P], F32, name="identity", tag="w1_raw1", align_bytes=64)
         make_identity(nc, identity[:])
         pairs = [keep.tile([P, T, 2], BF16, name="pair%d" % u, align_bytes=64) for u in range(2)]
-        for u, banks in enumerate(((0, 1, 2), (0, 1, 2))):
-            wide = [bank_tile([P, BANK], "wide%d%d" % (u, e), banks[e]) for e in range(2)]
-            order = [(0, 0), (1, 0), (0, 1), (0, 2), (0, 3), (1, 3), (1, 2), (1, 1)]
-            if u == 1:
-                order = sorted(order, key=lambda step: step[0])
-            for n, (e, s) in enumerate(order):
-                last = (e, s) in ((0, 3), (1, 1))
-                first_pass(wide[e][:], u, e, s, 0, BANK, last)
-                if last:
+        for u, order in enumerate((PAIR0_ORDER, sorted(PAIR0_ORDER, key=lambda step: step[0]))):
+            wide = [bank_tile([P, BANK], "wide%d%d" % (u, e), e) for e in range(2)]
+            closing = {e: s for e, s in order}
+            for e, s in order:
+                first_pass(wide[e][:], u, e, s, 0, BANK, s == closing[e])
+                if s == closing[e]:
                     nc.scalar.activation(out=pairs[u][:, 0:BANK, e], in_=wide[e][:], func=GELU)
-            last_tokens(u, banks[2])
+            last_tokens(u, 2)
 
         gathered = keep.tile([P, 2 * S], U32, name="gathered", align_bytes=64)
         for u, widths in enumerate(GATHERS):
@@ -257,19 +257,18 @@ def tile_moe_sup_lin_gelu_kernel(
             nc.scalar.copy(out=total[:], in_=turned_back[:])
             nc.scalar.dma_start(out=out[0:P, lo:hi], in_=total[:])
 
-        def add_and_store(products, at, lo, hi):
+        def add_and_store(products, first, lo, hi):
             total = keep.tile([P, hi - lo], F32, name="total1_%d" % lo)
-            cols = slice(at, at + hi - lo)
+            cols = slice(lo - first, hi - first)
             nc.vector.tensor_tensor(total[:], products[0][:, cols], products[1][:, cols], ADD)
             nc.sync.dma_start(out=out[P : 2 * P, lo:hi], in_=total[:])
 
-        early_sum, first_gather = BLOCK1_CUTS
-        head = product_tiles("head", first_gather)
-        tail = product_tiles("tail", T - first_gather)
+        head = product_tiles("head", HEAD_TOKENS)
+        tail = product_tiles("tail", T - HEAD_TOKENS)
         for r in range(2):
-            gather_product(head[r], 1, r, 0, first_gather)
-        gather_product(tail[0], 1, 0, first_gather, T)
-        add_and_store(head, 0, 0, early_sum)
-        gather_product(tail[1], 1, 1, first_gather, T)
-        add_and_store(head, early_sum, early_sum, first_gather)
-        add_and_store(tail, 0, first_gather, T)
+            gather_product(head[r], 1, r, 0, HEAD_TOKENS)
+        gather_product(tail[0], 1, 0, HEAD_TOKENS, T)
+        add_and_store(head, 0, 0, EARLY_SUMS)
+        gather_product(tail[1], 1, 1, HEAD_TOKENS, T)
+        add_and_store(head, 0, EARLY_SUMS, HEAD_TOKENS)
+        add_and_store(tail, HEAD_TOKENS, HEAD_TOKENS, T)

@@ -30,7 +30,7 @@ CHUNKS_BY_SCALAR = 4
 BLOCK0_PIECES = ((0, 384), (384, 640))
 HEAD_TOKENS = 448
 EARLY_SUMS = 320
-PAIR0_ORDER = ((0, 0), (1, 0), (0, 1), (0, 2), (0, 3), (1, 3), (1, 2), (1, 1))
+PAIR0_ORDER = ((0, 0), (1, 0), (0, 1), (1, 1), (0, 2), (0, 3), (1, 3), (1, 2))
 WARM_UP = (512, 512, 256)
 
 
@@ -212,7 +212,7 @@ def tile_moe_sup_lin_gelu_kernel(
                 expert(acc[:, at : at + C], 0, c, at)
             block0.append(acc)
         for c, acc in enumerate(block0):
-            empty = nc.scalar.copy if c < CHUNKS_BY_SCALAR else nc.vector.tensor_copy
+            empty = nc.vector.tensor_copy if c == 3 else nc.scalar.copy
             empty(out=y[0][:, starts[c] : starts[c + 1]], in_=acc[:])
 
         block1 = [

@@ -32,6 +32,7 @@ HEAD_TOKENS = 448
 EARLY_SUMS = 320
 PAIR0_ORDER = ((0, 0), (1, 0), (0, 1), (1, 1), (0, 2), (0, 3), (1, 3), (1, 2))
 WARM_UP = (512, 512, 256)
+PLANE_TOKENS = 320
 
 
 def tile_moe_sup_lin_gelu_kernel(
@@ -80,7 +81,8 @@ def tile_moe_sup_lin_gelu_kernel(
         load_w1(1)
         load_x(2, 3, 0, BANK)
         load_x(3, 4, 0, BANK)
-        load_x(0, PASSES, BANK, T)
+        load_x(0, 2, BANK, T)
+        load_x(2, PASSES, BANK, T)
 
         w1_grouped = {}
         w1_scales_grouped = {}
@@ -113,11 +115,15 @@ def tile_moe_sup_lin_gelu_kernel(
 
         w2_scales_sb = keep.tile([P, E, N], U8, name="w2_scales_sb", align_bytes=64)
         nc.vector.memset(w2_scales_sb[:].bitcast(I32), 0)
-        w2_sb = keep.tile([P, E, N], U32, name="w2_sb", align_bytes=64)
-        nc.sync.dma_start(out=w2_sb[:].bitcast(I32), in_=w2_words.rearrange("e s p n d -> p (e s) (n d)").bitcast(I32))
         load_scale_rows(w2_scales_sb, w2_scales.rearrange("e s (q j) n -> j q (e s) n", j=4))
         pos_sb = [keep.tile([P, T // LIST], U16, name="pos%d_sb" % (r + 1)) for r in range(2)]
         nc.sync.dma_start(pos_sb[0][:], pos1)
+        w2_rows = w2_words.rearrange("e s p n d -> p (e s) (n d)").bitcast(I32)
+        w2_sb = []
+        for lo in range(0, E, E // 2):
+            half = keep.tile([P, E // 2, N], U32, name="w2_sb%d" % lo, align_bytes=64)
+            nc.sync.dma_start(out=half[:].bitcast(I32), in_=w2_rows[:, lo : lo + E // 2, :])
+            w2_sb.extend(half[:, e, :] for e in range(E // 2))
         nc.sync.dma_start(pos_sb[1][:], pos2)
         gate_sb = keep.tile([P, 2, T], F32, name="gate_sb")
         nc.sync.dma_start(out=gate_sb[:], in_=gate.rearrange("r p t -> p r t"))
@@ -155,13 +161,19 @@ def tile_moe_sup_lin_gelu_kernel(
         identity = keep.tile([P, P], F32, name="identity", tag="w1_raw1", align_bytes=64)
         make_identity(nc, identity[:])
         pairs = [keep.tile([P, T, 2], BF16, name="pair%d" % u, align_bytes=64) for u in range(2)]
+        planes = keep.tile([P, 2, PLANE_TOKENS], BF16, name="planes", align_bytes=64)
         for u, order in enumerate((PAIR0_ORDER, sorted(PAIR0_ORDER, key=lambda step: step[0]))):
             wide = [bank_tile([P, BANK], "wide%d%d" % (u, e), e) for e in range(2)]
             closing = {e: s for e, s in order}
             for e, s in order:
                 first_pass(wide[e][:], u, e, s, 0, BANK, s == closing[e])
                 if s == closing[e]:
-                    nc.scalar.activation(out=pairs[u][:, 0:BANK, e], in_=wide[e][:], func=GELU)
+                    split = PLANE_TOKENS if u == 0 else 0
+                    if split:
+                        nc.scalar.activation(out=planes[:, e, :], in_=wide[e][:, 0:split], func=GELU)
+                    nc.scalar.activation(out=pairs[u][:, split:BANK, e], in_=wide[e][:, split:BANK], func=GELU)
+            if u == 0:
+                nc.vector.tensor_copy(out=pairs[0][:, 0:PLANE_TOKENS, :], in_=planes[:].rearrange("p e t -> p t e"))
             last_tokens(u, 2)
 
         gathered = keep.tile([P, 2 * S], U32, name="gathered", align_bytes=64)
@@ -184,7 +196,7 @@ def tile_moe_sup_lin_gelu_kernel(
             which = (starts[c] + at) // C
             nc.tensor.matmul_mx(
                 out=acc,
-                lhsT=w2_sb[:, which, b * P : (b + 1) * P].bitcast(FP8X4),
+                lhsT=w2_sb[which][:, b * P : (b + 1) * P].bitcast(FP8X4),
                 lhsT_scale=w2_scales_sb[:, which, b * P : (b + 1) * P],
                 rhs=codes[:, at : at + C].bitcast(FP8X4),
                 rhs_scale=scales[:, at : at + C],

@@ -25,11 +25,11 @@ BANK = 512
 LIST = 16
 
 GATHERS = ((448, 448, 384), (256, 256, 256, 256, 256))
-CHUNKS = (256, 256, 256, 256, 128, 128)
+CHUNKS = (256, 256, 256, 256, 128, 64, 64)
 CHUNKS_BY_SCALAR = 4
 BLOCK0_PIECES = ((0, 384), (384, 640))
-HEAD_TOKENS = 448
-EARLY_SUMS = 320
+HEAD_TOKENS = 512
+EARLY_SUMS = 256
 PAIR0_ORDER = ((0, 0), (1, 0), (0, 1), (1, 1), (0, 2), (0, 3), (1, 3), (1, 2))
 WARM_UP = (512, 512, 256)
 PLANE_TOKENS = 320
@@ -158,8 +158,9 @@ def tile_moe_sup_lin_gelu_kernel(
                     first_pass(acc[:, e, :], u, e, s, BANK, T, s == PASSES - 1)
             nc.scalar.activation(out=pairs[u][:, BANK:T, :], in_=acc[:].rearrange("p e t -> p t e"), func=GELU)
 
-        identity = keep.tile([P, P], F32, name="identity", tag="w1_raw1", align_bytes=64)
-        make_identity(nc, identity[:])
+        identity = keep.tile([P, P], F32, name="identity", align_bytes=64)
+        nc.vector.memset(identity[:], 0.0)
+        make_identity(nc, identity[:], nomemset=True)
         pairs = [keep.tile([P, T, 2], BF16, name="pair%d" % u, align_bytes=64) for u in range(2)]
         planes = keep.tile([P, 2, PLANE_TOKENS], BF16, name="planes", align_bytes=64)
         for u, order in enumerate((PAIR0_ORDER, sorted(PAIR0_ORDER, key=lambda step: step[0]))):
@@ -176,16 +177,22 @@ def tile_moe_sup_lin_gelu_kernel(
                 nc.vector.tensor_copy(out=pairs[0][:, 0:PLANE_TOKENS, :], in_=planes[:].rearrange("p e t -> p t e"))
             last_tokens(u, 2)
 
-        gathered = keep.tile([P, 2 * S], U32, name="gathered", align_bytes=64)
-        for u, widths in enumerate(GATHERS):
+        gathered = keep.tile([P, 3072], U32, name="gathered", align_bytes=64)
+
+        def place(u, slot):
+            return slot if u == 0 else S + slot % 768
+
+        def gather_words(u, pieces):
             window = pairs[u][:].rearrange("p t e -> p (t e)").bitcast(U32)
-            lo = 0
-            for width in widths:
+            for n in pieces:
+                lo = sum(GATHERS[u][:n])
+                hi = lo + GATHERS[u][n]
                 nc.vector.tensor_copy(
-                    out=gathered[:, u * S + lo : u * S + lo + width],
-                    in_=window.indirect(offs_sb[:, lo // LIST : (lo + width) // LIST]),
+                    out=gathered[:, place(u, lo) : place(u, lo) + hi - lo], in_=window.indirect(offs_sb[:, lo // LIST : hi // LIST])
                 )
-                lo = lo + width
+
+        gather_words(0, range(3))
+        gather_words(1, range(3))
 
         y = [keep.tile([P, S], F32, name="y%d" % b) for b in range(2)]
         starts = [sum(CHUNKS[:c]) for c in range(len(CHUNKS) + 1)]
@@ -193,38 +200,43 @@ def tile_moe_sup_lin_gelu_kernel(
 
         def expert(acc, b, c, at):
             codes, scales = quantised[c]
+            cols = slice(at, min(at + C, CHUNKS[c]))
             which = (starts[c] + at) // C
             nc.tensor.matmul_mx(
                 out=acc,
                 lhsT=w2_sb[which][:, b * P : (b + 1) * P].bitcast(FP8X4),
                 lhsT_scale=w2_scales_sb[:, which, b * P : (b + 1) * P],
-                rhs=codes[:, at : at + C].bitcast(FP8X4),
-                rhs_scale=scales[:, at : at + C],
+                rhs=codes[:, cols].bitcast(FP8X4),
+                rhs_scale=scales[:, cols],
                 start=True,
                 stop=True,
             )
 
-        block0_banks = (5, 6, 0, 1, 2, 3)
+        block0_banks = (5, 6, 0, 7, 1, 2, 3)
         block0 = []
         for c, width in enumerate(CHUNKS):
-            woven = keep.tile([P, width, 2], U32, name="woven%d" % c, align_bytes=64)
-            nc.scalar.copy(
-                out=woven[:], in_=gathered[:].rearrange("p (u j) -> p j u", u=2)[:, starts[c] : starts[c + 1], :]
-            )
+            woven = keep.tile([P, width, 2], U32, name="woven%d" % c, align_bytes=64)[:]
+            apart = place(1, starts[c]) - starts[c]
+            both = gathered[:, starts[c] : starts[c] + 2 * apart].rearrange("p (u j) -> p j u", u=2)
+            nc.scalar.copy(out=woven, in_=both[:, 0:width, :])
+            if c == 1:
+                gather_words(1, (4,))
             codes = keep.tile([P, width], U32, name="codes%d" % c, align_bytes=64)
             scales = keep.tile([P, width], U8, name="scales%d" % c, align_bytes=64)
             nc.vector.quantize_mx(
                 out=codes[:].bitcast(FP8X4),
                 scales=scales[:],
-                in_=woven[:].rearrange("p j u -> p (j u)").bitcast(BF16),
+                in_=woven.rearrange("p j u -> p (j u)").bitcast(BF16),
             )
             quantised.append((codes, scales))
+            if c == 0:
+                gather_words(1, (3,))
             acc = bank_tile([P, width], "block0_%d" % c, block0_banks[c])
             for at in range(0, width, C):
-                expert(acc[:, at : at + C], 0, c, at)
+                expert(acc[:, at : min(at + C, width)], 0, c, at)
             block0.append(acc)
         for c, acc in enumerate(block0):
-            empty = nc.vector.tensor_copy if c == 3 else nc.scalar.copy
+            empty = nc.vector.tensor_copy if c in (2, 4) else nc.scalar.copy
             empty(out=y[0][:, starts[c] : starts[c + 1]], in_=acc[:])
 
         block1 = [
@@ -234,7 +246,7 @@ def tile_moe_sup_lin_gelu_kernel(
         for c, width in enumerate(CHUNKS):
             for at in range(0, width, C):
                 slot = starts[c] + at
-                expert(block1[slot // BANK][:, slot % BANK : slot % BANK + C], 1, c, at)
+                expert(block1[slot // BANK][:, slot % BANK : slot % BANK + min(C, width)], 1, c, at)
         for k, acc in enumerate(block1):
             nc.scalar.copy(out=y[1][:, k * BANK : min((k + 1) * BANK, S)], in_=acc[:])
 

@@ -1,7 +1,6 @@
 from contextlib import ExitStack
 
 import concourse.mybir as mybir
-from concourse.masks import make_identity
 
 K, T, E, C, H, N = 2048, 640, 10, 128, 512, 256
 S = E * C
@@ -16,6 +15,7 @@ U8 = mybir.dt.uint8
 FP8X4 = mybir.dt.float8_e4m3fn_x4
 FP4X4 = mybir.dt.float4_e2m1fn_x4
 GELU = mybir.ActivationFunctionType.Gelu_apprx_tanh
+COPY = mybir.ActivationFunctionType.Copy
 MULT = mybir.AluOpType.mult
 ADD = mybir.AluOpType.add
 
@@ -27,7 +27,7 @@ LIST = 16
 GATHERS = ((448, 448, 384), (256, 256, 256, 256, 256))
 CHUNKS = (256, 256, 256, 256, 128, 64, 64)
 CHUNKS_BY_SCALAR = 4
-BLOCK0_PIECES = ((0, 384), (384, 640))
+PLAIN_TOKENS = 256
 HEAD_TOKENS = 512
 EARLY_SUMS = 256
 PAIR0_ORDER = ((0, 0), (1, 0), (0, 1), (1, 1), (0, 2), (0, 3), (1, 3), (1, 2))
@@ -158,9 +158,6 @@ def tile_moe_sup_lin_gelu_kernel(
                     first_pass(acc[:, e, :], u, e, s, BANK, T, s == PASSES - 1)
             nc.scalar.activation(out=pairs[u][:, BANK:T, :], in_=acc[:].rearrange("p e t -> p t e"), func=GELU)
 
-        identity = keep.tile([P, P], F32, name="identity", align_bytes=64)
-        nc.vector.memset(identity[:], 0.0)
-        make_identity(nc, identity[:], nomemset=True)
         pairs = [keep.tile([P, T, 2], BF16, name="pair%d" % u, align_bytes=64) for u in range(2)]
         planes = keep.tile([P, 2, PLANE_TOKENS], BF16, name="planes", align_bytes=64)
         for u, order in enumerate((PAIR0_ORDER, sorted(PAIR0_ORDER, key=lambda step: step[0]))):
@@ -239,6 +236,13 @@ def tile_moe_sup_lin_gelu_kernel(
             empty = nc.vector.tensor_copy if c in (2, 4) else nc.scalar.copy
             empty(out=y[0][:, starts[c] : starts[c + 1]], in_=acc[:])
 
+        def gather_plain(b, lo, hi):
+            plain = keep.tile([P, hi - lo], F32, name="plain%d_%d" % (b, lo))
+            nc.scalar.activation(out=plain[:], in_=y[b][:].indirect(pos_sb[0][:, lo // LIST : hi // LIST]), func=COPY)
+            return plain
+
+        plain0 = gather_plain(0, 0, PLAIN_TOKENS)
+
         block1 = [
             bank_tile([P, min(BANK, S - lo)], "block1_%d" % lo, bank)
             for lo, bank in zip(range(0, S, BANK), block0_banks[-3:])
@@ -250,49 +254,32 @@ def tile_moe_sup_lin_gelu_kernel(
         for k, acc in enumerate(block1):
             nc.scalar.copy(out=y[1][:, k * BANK : min((k + 1) * BANK, S)], in_=acc[:])
 
-        def product_tiles(name, width):
-            return [keep.tile([P, width], F32, name="%s%d" % (name, r)) for r in range(2)]
+        plain_head = gather_plain(1, 0, HEAD_TOKENS)
+        plain_tail = gather_plain(1, HEAD_TOKENS, T)
 
-        def gather_product(product, b, r, lo, hi):
+        products = [[keep.tile([P, T], F32, name="product%d%d" % (b, r)) for r in range(2)] for b in range(2)]
+
+        def gather_product(b, r, lo, hi):
             picked = y[b][:].indirect(pos_sb[r][:, lo // LIST : hi // LIST])
-            nc.vector.tensor_tensor(product[:], picked, gate_sb[:, r, lo:hi], MULT)
+            nc.vector.tensor_tensor(products[b][r][:, lo:hi], picked, gate_sb[:, r, lo:hi], MULT)
 
-        for n, (lo, hi) in enumerate(BLOCK0_PIECES):
-            products = product_tiles("product0_%d_" % n, hi - lo)
-            for r in range(2):
-                gather_product(products[r], 0, r, lo, hi)
-            turned_sum = bank_tile([P, hi - lo], "turned_sum%d" % n, block0_banks[-1 - n])
-            for at in range(0, hi - lo, P):
-                for r in range(2):
-                    nc.tensor.matmul(
-                        turned_sum[:, at : at + P],
-                        lhsT=products[r][:, at : at + P],
-                        rhs=identity[:],
-                        is_transpose=True,
-                        start=(r == 0),
-                        stop=(r == 1),
-                    )
-            turned = keep.tile([P, hi - lo], F32, name="turned%d" % n)
-            nc.scalar.copy(out=turned[:], in_=turned_sum[:])
-            turned_back = bank_tile([P, hi - lo], "turned_back%d" % n, 4 + n)
-            for at in range(0, hi - lo, P):
-                nc.tensor.transpose(turned_back[:, at : at + P], turned[:, at : at + P], identity[:])
-            total = keep.tile([P, hi - lo], F32, name="total%d" % n)
-            nc.scalar.copy(out=total[:], in_=turned_back[:])
-            nc.scalar.dma_start(out=out[0:P, lo:hi], in_=total[:])
+        def plain_product(plain, b, lo, hi):
+            nc.vector.tensor_tensor(products[b][0][:, lo:hi], plain[:], gate_sb[:, 0, lo:hi], MULT)
 
-        def add_and_store(products, first, lo, hi):
-            total = keep.tile([P, hi - lo], F32, name="total1_%d" % lo)
-            cols = slice(lo - first, hi - first)
-            nc.vector.tensor_tensor(total[:], products[0][:, cols], products[1][:, cols], ADD)
-            nc.sync.dma_start(out=out[P : 2 * P, lo:hi], in_=total[:])
+        def add_and_store(b, lo, hi):
+            total = keep.tile([P, hi - lo], F32, name="total%d_%d" % (b, lo))
+            nc.vector.tensor_tensor(total[:], products[b][0][:, lo:hi], products[b][1][:, lo:hi], ADD)
+            nc.sync.dma_start(out=out[b * P : (b + 1) * P, lo:hi], in_=total[:])
 
-        head = product_tiles("head", HEAD_TOKENS)
-        tail = product_tiles("tail", T - HEAD_TOKENS)
-        for r in range(2):
-            gather_product(head[r], 1, r, 0, HEAD_TOKENS)
-        gather_product(tail[0], 1, 0, HEAD_TOKENS, T)
-        add_and_store(head, 0, 0, EARLY_SUMS)
-        gather_product(tail[1], 1, 1, HEAD_TOKENS, T)
-        add_and_store(head, 0, EARLY_SUMS, HEAD_TOKENS)
-        add_and_store(tail, HEAD_TOKENS, HEAD_TOKENS, T)
+        gather_product(0, 1, 0, T)
+        plain_product(plain0, 0, 0, PLAIN_TOKENS)
+        gather_product(0, 0, PLAIN_TOKENS, T)
+        add_and_store(0, 0, PLAIN_TOKENS)
+        add_and_store(0, PLAIN_TOKENS, T)
+        gather_product(1, 1, 0, HEAD_TOKENS)
+        plain_product(plain_head, 1, 0, HEAD_TOKENS)
+        gather_product(1, 1, HEAD_TOKENS, T)
+        add_and_store(1, 0, EARLY_SUMS)
+        plain_product(plain_tail, 1, HEAD_TOKENS, T)
+        add_and_store(1, EARLY_SUMS, HEAD_TOKENS)
+        add_and_store(1, HEAD_TOKENS, T)

@@ -27,7 +27,7 @@ LIST = 16
 GATHERS = ((448, 448, 384), (256, 256, 256, 256, 256))
 CHUNKS = (256, 256, 256, 256, 128, 64, 64)
 CHUNKS_BY_SCALAR = 4
-PLAIN_TOKENS = 256
+PLAIN_TOKENS = 384
 HEAD_TOKENS = 512
 EARLY_SUMS = 256
 PAIR0_ORDER = ((0, 0), (1, 0), (0, 1), (1, 1), (0, 2), (0, 3), (1, 3), (1, 2))
@@ -236,12 +236,14 @@ def tile_moe_sup_lin_gelu_kernel(
             empty = nc.vector.tensor_copy if c in (2, 4) else nc.scalar.copy
             empty(out=y[0][:, starts[c] : starts[c + 1]], in_=acc[:])
 
-        def gather_plain(b, lo, hi):
-            plain = keep.tile([P, hi - lo], F32, name="plain%d_%d" % (b, lo))
-            nc.scalar.activation(out=plain[:], in_=y[b][:].indirect(pos_sb[0][:, lo // LIST : hi // LIST]), func=COPY)
+        def gather_plain(b, choices, lo, hi):
+            plain = keep.tile([P, choices, hi - lo], F32, name="plain%d_%d" % (b, lo))
+            for r in range(choices):
+                picked = y[b][:].indirect(pos_sb[r][:, lo // LIST : hi // LIST])
+                nc.scalar.activation(out=plain[:, r, :], in_=picked, func=COPY)
             return plain
 
-        plain0 = gather_plain(0, 0, PLAIN_TOKENS)
+        plain0 = gather_plain(0, 1, 0, PLAIN_TOKENS)
 
         block1 = [
             bank_tile([P, min(BANK, S - lo)], "block1_%d" % lo, bank)
@@ -254,32 +256,33 @@ def tile_moe_sup_lin_gelu_kernel(
         for k, acc in enumerate(block1):
             nc.scalar.copy(out=y[1][:, k * BANK : min((k + 1) * BANK, S)], in_=acc[:])
 
-        plain_head = gather_plain(1, 0, HEAD_TOKENS)
-        plain_tail = gather_plain(1, HEAD_TOKENS, T)
+        plain_a = gather_plain(1, 1, 0, EARLY_SUMS)
+        plain_b = gather_plain(1, 1, EARLY_SUMS, HEAD_TOKENS)
+        plain_tail = gather_plain(1, 2, HEAD_TOKENS, T)
 
-        products = [[keep.tile([P, T], F32, name="product%d%d" % (b, r)) for r in range(2)] for b in range(2)]
+        products = [keep.tile([P, 2, T], F32, name="products%d" % b) for b in range(2)]
 
         def gather_product(b, r, lo, hi):
             picked = y[b][:].indirect(pos_sb[r][:, lo // LIST : hi // LIST])
-            nc.vector.tensor_tensor(products[b][r][:, lo:hi], picked, gate_sb[:, r, lo:hi], MULT)
+            nc.vector.tensor_tensor(products[b][:, r, lo:hi], picked, gate_sb[:, r, lo:hi], MULT)
 
-        def plain_product(plain, b, lo, hi):
-            nc.vector.tensor_tensor(products[b][0][:, lo:hi], plain[:], gate_sb[:, 0, lo:hi], MULT)
+        def plain_product(plain, b, choices, lo, hi):
+            nc.vector.tensor_tensor(products[b][:, 0:choices, lo:hi], plain[:], gate_sb[:, 0:choices, lo:hi], MULT)
 
         def add_and_store(b, lo, hi):
             total = keep.tile([P, hi - lo], F32, name="total%d_%d" % (b, lo))
-            nc.vector.tensor_tensor(total[:], products[b][0][:, lo:hi], products[b][1][:, lo:hi], ADD)
+            nc.vector.tensor_tensor(total[:], products[b][:, 0, lo:hi], products[b][:, 1, lo:hi], ADD)
             nc.sync.dma_start(out=out[b * P : (b + 1) * P, lo:hi], in_=total[:])
 
         gather_product(0, 1, 0, T)
-        plain_product(plain0, 0, 0, PLAIN_TOKENS)
+        plain_product(plain0, 0, 1, 0, PLAIN_TOKENS)
         gather_product(0, 0, PLAIN_TOKENS, T)
         add_and_store(0, 0, PLAIN_TOKENS)
         add_and_store(0, PLAIN_TOKENS, T)
         gather_product(1, 1, 0, HEAD_TOKENS)
-        plain_product(plain_head, 1, 0, HEAD_TOKENS)
-        gather_product(1, 1, HEAD_TOKENS, T)
+        plain_product(plain_a, 1, 1, 0, EARLY_SUMS)
+        plain_product(plain_b, 1, 1, EARLY_SUMS, HEAD_TOKENS)
         add_and_store(1, 0, EARLY_SUMS)
-        plain_product(plain_tail, 1, HEAD_TOKENS, T)
+        plain_product(plain_tail, 1, 2, HEAD_TOKENS, T)
         add_and_store(1, EARLY_SUMS, HEAD_TOKENS)
         add_and_store(1, HEAD_TOKENS, T)

from contextlib import ExitStack

import concourse.mybir as mybir

K, T, E, C, H, N = 2048, 640, 10, 128, 512, 256
S = E * C
FLOPS = 2 * K * H * T + 2 * H * N * S

F32 = mybir.dt.float32
BF16 = mybir.dt.bfloat16
I32 = mybir.dt.int32
U32 = mybir.dt.uint32
U16 = mybir.dt.uint16
U8 = mybir.dt.uint8
FP8X4 = mybir.dt.float8_e4m3fn_x4
FP4X4 = mybir.dt.float4_e2m1fn_x4
GELU = mybir.ActivationFunctionType.Gelu_apprx_tanh
COPY = mybir.ActivationFunctionType.Copy
MULT = mybir.AluOpType.mult
ADD = mybir.AluOpType.add

P = 128
PASSES = K // 512
BANK = 512
LIST = 16

GATHERS = ((448, 448, 384), (256, 256, 256, 256, 256))
CHUNKS = (256, 256, 256, 256, 128, 64, 64)
CHUNKS_BY_SCALAR = 4
PLAIN_TOKENS = 384
HEAD_TOKENS = 512
EARLY_SUMS = 256
PAIR0_ORDER = ((0, 0), (1, 0), (0, 1), (1, 1), (0, 2), (0, 3), (1, 3), (1, 2))
WARM_UP = (512, 512, 256)
PLANE_TOKENS = 320


def tile_moe_sup_lin_gelu_kernel(
    tc, x_words, x_scales, w1_words, w1_scales, w2_words, w2_scales, gate, offs, pos1, pos2, out
):
    nc = tc.nc
    with ExitStack() as ctx:
        keep = ctx.enter_context(tc.tile_pool(name="keep", bufs=1))
        psum = ctx.enter_context(tc.psum_pool(name="psum", bufs=1))

        def bank_tile(shape, name, bank):
            return psum.tile(shape, F32, name=name, tag="bank%d" % bank)

        def load_scale_rows(plane, rows):
            for j in range(4):
                nc.sync.dma_start(out=plane[j:P:32].bitcast(I32), in_=rows[j].bitcast(I32))

        w1_scales_raw = keep.tile([P, PASSES, H], U8, name="w1_scales_raw", align_bytes=64)
        x_scales_sb = keep.tile([P, PASSES, T], U8, name="x_scales_sb", align_bytes=64)
        nc.vector.memset(w1_scales_raw[:].bitcast(I32), 0)
        nc.vector.memset(x_scales_sb[:].bitcast(I32), 0)

        w1_rows = w1_words.rearrange("s p b -> p s b").bitcast(I32)
        x_rows = x_words.rearrange("s p t d -> p s (t d)").bitcast(I32)
        w1_raw = []
        x_tiles = {}

        def load_w1(half):
            raw = keep.tile([P, 2, 2 * H], U8, name="w1_raw%d" % half, tag="w1_raw%d" % half, align_bytes=64)
            nc.sync.dma_start(out=raw[:].bitcast(I32), in_=w1_rows[:, 2 * half : 2 * half + 2, :])
            w1_raw.append(raw)

        def load_x(s0, s1, lo, hi):
            part = keep.tile([P, s1 - s0, hi - lo], U32, name="x%d_%d" % (s0, lo), align_bytes=64)
            nc.sync.dma_start(out=part[:].bitcast(I32), in_=x_rows[:, s0:s1, lo:hi])
            for s in range(s0, s1):
                x_tiles[(s, lo)] = part[:, s - s0, :]

        load_x(0, 1, 0, BANK)
        offs_sb = keep.tile([P, S // LIST], U16, name="offs_sb")
        nc.sync.dma_start(offs_sb[:], offs)
        load_scale_rows(w1_scales_raw, w1_scales.rearrange("s (q j) i -> j q s i", j=4))
        load_w1(0)
        load_x(1, 2, 0, BANK)
        load_scale_rows(x_scales_sb, x_scales.rearrange("s (q j) t -> j q s t", j=4))
        load_w1(1)
        load_x(2, 3, 0, BANK)
        load_x(3, 4, 0, BANK)
        load_x(0, 2, BANK, T)
        load_x(2, PASSES, BANK, T)

        w1_grouped = {}
        w1_scales_grouped = {}

        def regroup_scales(u):
            grouped = keep.tile([P, PASSES, 2, P], U8, name="w1_scales%d" % u, align_bytes=64)
            nc.vector.tensor_copy(
                out=grouped[:],
                in_=w1_scales_raw[:].rearrange("p s (m d) -> p s d m", d=4)[:, :, 2 * u : 2 * u + 2, :],
            )
            w1_scales_grouped[u] = grouped

        def regroup_words(u, s0, s1):
            grouped = keep.tile([P, s1 - s0, 2 * 2 * P], U8, name="w1_words%d%d" % (u, s0), align_bytes=64)
            source = w1_raw[s0 // 2][:, s0 % 2 : s0 % 2 + s1 - s0, :].bitcast(U16).rearrange("p s (m d) -> p s d m", d=4)
            nc.vector.tensor_copy(
                out=grouped[:].bitcast(U16).rearrange("p s (e m) -> p s e m", e=2),
                in_=source[:, :, 2 * u : 2 * u + 2, :],
            )
            for s in range(s0, s1):
                w1_grouped[(u, s)] = grouped[:, s - s0, :]

        regroup_scales(0)
        regroup_scales(1)
        regroup_words(0, 0, 1)
        regroup_words(0, 1, 2)
        regroup_words(0, 2, 4)
        regroup_words(1, 0, 2)
        regroup_words(1, 2, 4)

        w2_scales_sb = keep.tile([P, E, N], U8, name="w2_scales_sb", align_bytes=64)
        nc.vector.memset(w2_scales_sb[:].bitcast(I32), 0)
        load_scale_rows(w2_scales_sb, w2_scales.rearrange("e s (q j) n -> j q (e s) n", j=4))
        pos_sb = [keep.tile([P, T // LIST], U16, name="pos%d_sb" % (r + 1)) for r in range(2)]
        nc.sync.dma_start(pos_sb[0][:], pos1)
        w2_rows = w2_words.rearrange("e s p n d -> p (e s) (n d)").bitcast(I32)
        w2_sb = []
        for lo in range(0, E, E // 2):
            half = keep.tile([P, E // 2, N], U32, name="w2_sb%d" % lo, align_bytes=64)
            nc.sync.dma_start(out=half[:].bitcast(I32), in_=w2_rows[:, lo : lo + E // 2, :])
            w2_sb.extend(half[:, e, :] for e in range(E // 2))
        nc.sync.dma_start(pos_sb[1][:], pos2)
        gate_sb = keep.tile([P, 2, T], F32, name="gate_sb")
        nc.sync.dma_start(out=gate_sb[:], in_=gate.rearrange("r p t -> p r t"))

        def first_pass(acc, u, e, s, lo, hi, last):
            nc.tensor.matmul_mx(
                out=acc,
                lhsT=w1_grouped[(u, s)][:, e * 2 * P : (e + 1) * 2 * P].bitcast(FP4X4),
                lhsT_scale=w1_scales_grouped[u][:, s, e, :],
                rhs=x_tiles[(s, lo)].bitcast(FP8X4),
                rhs_scale=x_scales_sb[:, s, lo:hi],
                start=(s == 0),
                stop=last,
            )

        warm = bank_tile([P, BANK], "warm", 7)
        for width in WARM_UP:
            nc.tensor.matmul_mx(
                out=warm[:, 0:width],
                lhsT=x_tiles[(0, 0)][:, 0:P].bitcast(FP8X4),
                lhsT_scale=w1_scales_raw[:, 0, 0:P],
                rhs=x_tiles[(0, 0)][:, 0:width].bitcast(FP8X4),
                rhs_scale=w1_scales_raw[:, 0, 0:width],
                start=True,
                stop=True,
            )

        def last_tokens(u, bank):
            acc = bank_tile([P, 2, P], "hidden%d" % u, bank)
            for e in range(2):
                for s in range(PASSES):
                    first_pass(acc[:, e, :], u, e, s, BANK, T, s == PASSES - 1)
            nc.scalar.activation(out=pairs[u][:, BANK:T, :], in_=acc[:].rearrange("p e t -> p t e"), func=GELU)

        pairs = [keep.tile([P, T, 2], BF16, name="pair%d" % u, align_bytes=64) for u in range(2)]
        planes = keep.tile([P, 2, PLANE_TOKENS], BF16, name="planes", align_bytes=64)
        for u, order in enumerate((PAIR0_ORDER, sorted(PAIR0_ORDER, key=lambda step: step[0]))):
            wide = [bank_tile([P, BANK], "wide%d%d" % (u, e), e) for e in range(2)]
            closing = {e: s for e, s in order}
            for e, s in order:
                first_pass(wide[e][:], u, e, s, 0, BANK, s == closing[e])
                if s == closing[e]:
                    split = PLANE_TOKENS if u == 0 else 0
                    if split:
                        nc.scalar.activation(out=planes[:, e, :], in_=wide[e][:, 0:split], func=GELU)
                    nc.scalar.activation(out=pairs[u][:, split:BANK, e], in_=wide[e][:, split:BANK], func=GELU)
            if u == 0:
                nc.vector.tensor_copy(out=pairs[0][:, 0:PLANE_TOKENS, :], in_=planes[:].rearrange("p e t -> p t e"))
            last_tokens(u, 2)

        gathered = keep.tile([P, 3072], U32, name="gathered", align_bytes=64)

        def place(u, slot):
            return slot if u == 0 else S + slot % 768

        def gather_words(u, pieces):
            window = pairs[u][:].rearrange("p t e -> p (t e)").bitcast(U32)
            for n in pieces:
                lo = sum(GATHERS[u][:n])
                hi = lo + GATHERS[u][n]
                nc.vector.tensor_copy(
                    out=gathered[:, place(u, lo) : place(u, lo) + hi - lo], in_=window.indirect(offs_sb[:, lo // LIST : hi // LIST])
                )

        gather_words(0, range(3))
        gather_words(1, range(3))

        y = [keep.tile([P, S], F32, name="y%d" % b) for b in range(2)]
        starts = [sum(CHUNKS[:c]) for c in range(len(CHUNKS) + 1)]
        quantised = []

        def expert(acc, b, c, at):
            codes, scales = quantised[c]
            cols = slice(at, min(at + C, CHUNKS[c]))
            which = (starts[c] + at) // C
            nc.tensor.matmul_mx(
                out=acc,
                lhsT=w2_sb[which][:, b * P : (b + 1) * P].bitcast(FP8X4),
                lhsT_scale=w2_scales_sb[:, which, b * P : (b + 1) * P],
                rhs=codes[:, cols].bitcast(FP8X4),
                rhs_scale=scales[:, cols],
                start=True,
                stop=True,
            )

        block0_banks = (5, 6, 0, 7, 1, 2, 3)
        block0 = []
        for c, width in enumerate(CHUNKS):
            woven = keep.tile([P, width, 2], U32, name="woven%d" % c, align_bytes=64)[:]
            apart = place(1, starts[c]) - starts[c]
            both = gathered[:, starts[c] : starts[c] + 2 * apart].rearrange("p (u j) -> p j u", u=2)
            nc.scalar.copy(out=woven, in_=both[:, 0:width, :])
            if c == 1:
                gather_words(1, (4,))
            codes = keep.tile([P, width], U32, name="codes%d" % c, align_bytes=64)
            scales = keep.tile([P, width], U8, name="scales%d" % c, align_bytes=64)
            nc.vector.quantize_mx(
                out=codes[:].bitcast(FP8X4),
                scales=scales[:],
                in_=woven.rearrange("p j u -> p (j u)").bitcast(BF16),
            )
            quantised.append((codes, scales))
            if c == 0:
                gather_words(1, (3,))
            acc = bank_tile([P, width], "block0_%d" % c, block0_banks[c])
            for at in range(0, width, C):
                expert(acc[:, at : min(at + C, width)], 0, c, at)
            block0.append(acc)
        for c, acc in enumerate(block0):
            empty = nc.vector.tensor_copy if c in (2, 4) else nc.scalar.copy
            empty(out=y[0][:, starts[c] : starts[c + 1]], in_=acc[:])

        def gather_plain(b, choices, lo, hi):
            plain = keep.tile([P, choices, hi - lo], F32, name="plain%d_%d" % (b, lo))
            for r in range(choices):
                picked = y[b][:].indirect(pos_sb[r][:, lo // LIST : hi // LIST])
                nc.scalar.activation(out=plain[:, r, :], in_=picked, func=COPY)
            return plain

        plain0 = gather_plain(0, 1, 0, PLAIN_TOKENS)

        block1 = [
            bank_tile([P, min(BANK, S - lo)], "block1_%d" % lo, bank)
            for lo, bank in zip(range(0, S, BANK), block0_banks[-3:])
        ]
        for c, width in enumerate(CHUNKS):
            for at in range(0, width, C):
                slot = starts[c] + at
                expert(block1[slot // BANK][:, slot % BANK : slot % BANK + min(C, width)], 1, c, at)
        for k, acc in enumerate(block1):
            nc.scalar.copy(out=y[1][:, k * BANK : min((k + 1) * BANK, S)], in_=acc[:])

        plain_a = gather_plain(1, 1, 0, EARLY_SUMS)
        plain_b = gather_plain(1, 1, EARLY_SUMS, HEAD_TOKENS)
        plain_tail = gather_plain(1, 2, HEAD_TOKENS, T)

        products = [keep.tile([P, 2, T], F32, name="products%d" % b) for b in range(2)]

        def gather_product(b, r, lo, hi):
            picked = y[b][:].indirect(pos_sb[r][:, lo // LIST : hi // LIST])
            nc.vector.tensor_tensor(products[b][:, r, lo:hi], picked, gate_sb[:, r, lo:hi], MULT)

        def plain_product(plain, b, choices, lo, hi):
            nc.vector.tensor_tensor(products[b][:, 0:choices, lo:hi], plain[:], gate_sb[:, 0:choices, lo:hi], MULT)

        def add_and_store(b, lo, hi):
            total = keep.tile([P, hi - lo], F32, name="total%d_%d" % (b, lo))
            nc.vector.tensor_tensor(total[:], products[b][:, 0, lo:hi], products[b][:, 1, lo:hi], ADD)
            nc.sync.dma_start(out=out[b * P : (b + 1) * P, lo:hi], in_=total[:])

        gather_product(0, 1, 0, T)
        plain_product(plain0, 0, 1, 0, PLAIN_TOKENS)
        gather_product(0, 0, PLAIN_TOKENS, T)
        add_and_store(0, 0, PLAIN_TOKENS)
        add_and_store(0, PLAIN_TOKENS, T)
        gather_product(1, 1, 0, HEAD_TOKENS)
        plain_product(plain_a, 1, 1, 0, EARLY_SUMS)
        plain_product(plain_b, 1, 1, EARLY_SUMS, HEAD_TOKENS)
        add_and_store(1, 0, EARLY_SUMS)
        plain_product(plain_tail, 1, 2, HEAD_TOKENS, T)
        add_and_store(1, EARLY_SUMS, HEAD_TOKENS)
        add_and_store(1, HEAD_TOKENS, T)
